import numpy as np, ml_dtypes
CORES = [6,14,22,30,38,134,142,150,158]
N = 9
def setup_inputs(rng):
    m = (rng.standard_normal((N, 128, 128), dtype=np.float32) / 11).astype(ml_dtypes.bfloat16)
    return {"m": m, "mt": m.transpose(0, 2, 1).copy()}
def setup_inputs_low(rng):
    d = setup_inputs(rng)
    for k in ("m", "mt"): d[k] = (d[k].astype(np.float32) * 0.125).astype(d[k].dtype)
    return d
def reference(m, mt):
    M = m.astype(np.float64); p = M[0]
    for r in range(1, N):
        p = p @ M[r]
    p = p.astype(ml_dtypes.bfloat16)
    return {"y": np.broadcast_to(p, (N, 128, 128))}

from concourse.bass import DstId, RemoteDMATransfer

D = 128
FAN = (3, 3)
ENGINES = (8, 8)


def _tree(lo, hi):
    if hi - lo == 1:
        return lo
    mid = (lo + hi) // 2
    return (_tree(lo, mid), _tree(mid, hi))


def _height(t):
    return 0 if isinstance(t, int) else 1 + max(_height(t[0]), _height(t[1]))


def _by_height(t, transposed, out):
    if isinstance(t, int):
        return
    out.setdefault(_height(t), []).append((t, transposed))
    _by_height(t[0], True, out)
    _by_height(t[1], False, out)


def _leaf_forms(t, transposed, out):
    if isinstance(t, int):
        out[t] = transposed
        return
    _leaf_forms(t[0], True, out)
    _leaf_forms(t[1], False, out)


def _steps():
    steps = []
    for s, f in enumerate(FAN):
        lev = {}
        _by_height(_tree(0, f), False, lev)
        for h in sorted(lev):
            steps.append((s, h, len(lev[h])))
    return steps


SCRATCH = {"out": ("sbuf", [D, D], "bfloat16")}
for _s, _f in enumerate(FAN):
    SCRATCH["in%d" % _s] = ("sbuf", [D, _f * D], "bfloat16")
for _i, (_s, _h, _w) in enumerate(_steps()):
    SCRATCH["ps%d" % _i] = ("psum", [D, 512], "float32")
    SCRATCH["tmp%d" % _i] = ("sbuf", [D, _w * D], "bfloat16")
SEMAPHORES = ["loaded", "sent", "mm", "cp", "stored"] + ["arr%d" % _s for _s in range(len(FAN))]


def _perms(n):
    if n == 0:
        return [[]]
    res = []
    for p in _perms(n - 1):
        for i in range(n):
            res.append(p[:i] + [n - 1] + p[i:])
    return sorted(res)


def _links(topo, a, b):
    return 1 if (topo.mates(a, b) or topo.same_plane(a, b)) else 2


def _match(topo, src, dst):
    best = None
    for p in _perms(len(src)):
        c = sum(_links(topo, src[i], dst[p[i]]) for i in range(len(src)))
        if best is None or c < best[0]:
            best = (c, p)
    return best[1]


def _pick(mask, n):
    got, bit = 0, 1
    while n:
        if mask & bit:
            got |= bit
            n -= 1
        bit <<= 1
    return got


def rank_program(g, core, T, topo):
    rank = T.rank_of(core)
    if rank is None:
        return
    cores = T.cores
    sem = T.sem
    n_rounds = len(FAN)

    size = [1]
    for f in FAN:
        size.append(size[-1] * f)
    child = [(rank % size[s + 1]) // size[s] for s in range(n_rounds)]
    forms = []
    for f in FAN:
        lf = {}
        _leaf_forms(_tree(0, f), False, lf)
        forms.append(lf)

    def slot(s, k):
        return T["in%d" % s][:, k * D:(k + 1) * D]

    g.sync.dma_start(slot(0, child[0]), (T.mt if forms[0][child[0]] else T.m)[:]).then_inc(sem.loaded, 16)

    n_mm, n_cp, n_sent, step = 0, 0, 0, 0
    for s in range(n_rounds):
        f, k, pos = FAN[s], child[s], rank % size[s]
        base = rank - rank % size[s + 1]
        mine = [cores[base + k * size[s] + i] for i in range(size[s])]
        dsts = []
        for k2 in range(f):
            if k2 != k:
                theirs = [cores[base + k2 * size[s] + i] for i in range(size[s])]
                dsts.append(theirs[_match(topo, mine, theirs)[pos]])
        mask = topo.mask(core, dsts[0])
        for d in dsts:
            assert topo.may_write(core, d)
            mask &= topo.mask(core, d)
        mask = _pick(mask, ENGINES[s])
        if s == 0:
            g.wait_ge(sem.loaded, 16)
        else:
            g.wait_ge(sem.cp, n_cp)
        ids = []
        for d in dsts:
            rid, pid = topo.addr(d, core)
            ids.append(DstId(rid=rid, pnc=pid))
        g.remote_dma_fused(
            [RemoteDMATransfer(dst_ids=ids, dma_engine_mask=mask, remote_sem=sem["arr%d" % s],
                               srcs=[slot(s, k)], dsts=[slot(s, k) for _ in dsts])],
            local_sem=sem.sent)
        n_sent += ENGINES[s]

        want_t = forms[s + 1][child[s + 1]] if s + 1 < n_rounds else False
        dest = slot(s + 1, child[s + 1]) if s + 1 < n_rounds else T.out[:]
        lev = {}
        tree = _tree(0, f)
        _by_height(tree, want_t, lev)
        where = {}
        for kk in range(f):
            where[kk] = slot(s, kk)
        if s == 0:
            g.tensor.wait_ge(sem.loaded, 16)
        g.tensor.wait_ge(sem["arr%d" % s], (f - 1) * ENGINES[s])
        for h in sorted(lev):
            ps, tmp = T["ps%d" % step], T["tmp%d" % step]
            if n_cp:
                g.tensor.wait_ge(sem.cp, n_cp)
            for i, (t, tr) in enumerate(lev[h]):
                left_t, right = where[t[0]], where[t[1]]
                o = ps[:, i * D:(i + 1) * D]
                if tr:
                    g.tensor.matmul(o, right, left_t, True, True).then_inc(sem.mm, 1)
                else:
                    g.tensor.matmul(o, left_t, right, True, True).then_inc(sem.mm, 1)
                n_mm += 1
                where[t] = tmp[:, i * D:(i + 1) * D]
            w = len(lev[h]) * D
            g.vector.wait_ge(sem.mm, n_mm)
            g.vector.tensor_copy(dest if t is tree else tmp[:, 0:w], ps[:, 0:w]).then_inc(sem.cp, 1)
            n_cp += 1
            step += 1

    g.sync.wait_ge(sem.cp, n_cp)
    g.sync.dma_start(T.y[:], T.out[:]).then_inc(sem.stored, 16)
    g.sync.wait_ge(sem.stored, 16)
    g.wait_ge(sem.sent, n_sent)
